import numpy as np
import ml_dtypes


def mxq(x, axis, fmt="e4m3"):
    dtype, down = {"e4m3": (ml_dtypes.float8_e4m3fn, 7), "e5m2": (ml_dtypes.float8_e5m2, 14)}[fmt]
    v = np.moveaxis(np.asarray(x, np.float32).astype(ml_dtypes.bfloat16).astype(np.float64), axis, -1)
    blocks = v.reshape(v.shape[:-1] + (-1, 32))
    amax = np.abs(blocks).max(-1, keepdims=True)
    byte = np.maximum(np.where(amax > 0, np.frexp(amax)[1] - 1 + 127, 0) - down, 1)
    scale = np.exp2(byte - 127.0)
    codes = (blocks / scale).astype(np.float32).astype(dtype).astype(np.float64)
    return np.moveaxis((codes * scale).reshape(v.shape), -1, axis)


WIDE = False


def mx_kscale(k):
    if not WIDE:
        return np.ones(k)
    levels = np.array([10, -10, 5, -5, 0])
    if k % 512:
        return np.exp2(np.random.permutation(np.resize(levels, k // 32))).repeat(32)
    a = np.empty((k // 512, 16))
    for p in range(k // 512):
        a[p, :8] = np.random.permutation(np.resize(levels, 8))
        for g in range(8):
            far = levels[np.abs(levels - a[p, g]) >= 10]
            a[p, g + 8] = far[np.random.randint(len(far))]
    return np.exp2(a.ravel()).repeat(32)


def f64(x):
    return np.asarray(x).astype(np.float64)


def striped(idx):
    return np.tile(idx.reshape(-1, 16).T, (8, 1)).astype(np.uint16)


def unstriped(offs):
    return offs[:16].T.reshape(-1).astype(np.int64)


E2M1 = np.array([0.0, 0.5, 1.0, 1.5, 2.0, 3.0, 4.0, 6.0, -0.0, -0.5, -1.0, -1.5, -2.0, -3.0, -4.0, -6.0])


def pack_weight(w, fmt):
    k, n = w.shape
    w = f64(np.asarray(w, np.float32).astype(ml_dtypes.bfloat16)).reshape(k // 32, 32, n)
    amax = np.abs(w).max(1)
    if fmt == "e4m3":
        byte = np.frexp(amax)[1] - 1 + 127 - 7
    else:
        mant, ex = np.frexp(amax / 6.0)
        byte = np.where(mant > 0.5, ex, ex - 1) + 127
    byte = np.clip(np.where(amax > 0, byte, 1), 1, 254)
    scaled = (w * np.exp2(127.0 - byte)[:, None, :]).reshape(k, n).astype(np.float32)
    by_word = np.ascontiguousarray(scaled.reshape(k // 512, 128, 4, n).transpose(0, 1, 3, 2))
    if fmt == "e4m3":
        words = by_word.astype(ml_dtypes.float8_e4m3fn).view(np.uint8)
    else:
        c = by_word.astype(ml_dtypes.float4_e2m1fn).view(np.uint8) & 0xF
        words = (c[..., 0::2] | (c[..., 1::2] << 4)).reshape(k // 512, 128, 2 * n)
    return np.ascontiguousarray(words), np.ascontiguousarray(byte.astype(np.uint8).reshape(k // 512, 16, n))


def unpack_weight(words, scales, fmt):
    g, _, n = scales.shape
    words = np.ascontiguousarray(words).reshape(g, 128, n, -1)
    if fmt == "e4m3":
        vals = words.view(ml_dtypes.float8_e4m3fn).astype(np.float64)
    else:
        nib = np.empty((g, 128, n, 4), np.uint8)
        nib[..., 0::2] = words & 0xF
        nib[..., 1::2] = words >> 4
        vals = E2M1[nib]
    vals = vals * np.repeat(np.exp2(scales.astype(np.float64) - 127.0), 8, axis=1)[..., None]
    return vals.transpose(0, 1, 3, 2).reshape(g * 512, n)


def gelu(v):
    return 0.5 * v * (1.0 + np.tanh(np.sqrt(2.0 / np.pi) * (v + 0.044715 * v**3)))


K, H, N, T, S, P, P2 = 1024, 512, 512, 4096, 2048, 1024, 512

def setup_inputs():
    n = np.random.standard_normal
    s = mx_kscale(K)[:, None]
    u = mx_kscale(H)[:, None]
    tab_words, tab_scales = pack_weight(n((K, T)) * s, "e4m3")
    wt_words, wt_scales = pack_weight(1.5 * n((K, H)) / np.sqrt(K) / s, "e2m1")
    return {
        "tab_words": tab_words,
        "tab_scales": tab_scales,
        "offs": striped(np.random.permutation(T)[:S]),
        "pos1": striped(np.random.permutation(S)[:P]),
        "pos2": striped(np.random.permutation(S)[:P]),
        "pos3": striped(np.random.permutation(P)[:P2]),
        "pos4": striped(np.random.permutation(S)[:P2]),
        "wp": (n((K, H)) / np.sqrt(K) / s).astype(np.float32),
        "wt_words": wt_words,
        "wt_scales": wt_scales,
        "gain": (np.exp(0.4 * n(H)) * u[:, 0]).astype(np.float32),
        "wo": (n((H, N)) / np.sqrt(H) / u * np.exp(0.4 * n(N))).astype(np.float32),
    }

def reference(tab_words, tab_scales, offs, pos1, pos2, pos3, pos4, wp, wt_words, wt_scales, gain, wo):
    v = unpack_weight(tab_words, tab_scales, "e4m3")[:, unstriped(offs)]
    wpq = mxq(f64(wp), 0, "e4m3")
    wt = unpack_weight(wt_words, wt_scales, "e2m1")
    h = (wpq.T @ v) + np.tanh(wt.T @ v)
    first = h[:, unstriped(pos1)]
    second = h[:, unstriped(pos2)]
    a1 = first * np.tanh(second) + first
    kept = a1[:, unstriped(pos3)]
    exhibit = h[:, unstriped(pos4)]
    a2 = f64(gain)[:, None] * np.maximum(kept, exhibit)
    aq = mxq(a2, 0, "e4m3")
    woq = mxq(f64(wo), 0, "e4m3")
    return woq.T @ aq

@@ -1,0 +1,275 @@
+from contextlib import ExitStack
+
+import concourse.mybir as mybir
+
+K, H, N, T, S, PAIRS, KEPT = 1024, 512, 512, 4096, 2048, 1024, 512
+FLOPS = 2 * 2 * K * H * S + 2 * H * N * KEPT
+
+F32 = mybir.dt.float32
+BF16 = mybir.dt.bfloat16
+I32 = mybir.dt.int32
+U32 = mybir.dt.uint32
+U16 = mybir.dt.uint16
+U8 = mybir.dt.uint8
+FP8X4 = mybir.dt.float8_e4m3fn_x4
+FP4X4 = mybir.dt.float4_e2m1fn_x4
+ACT = mybir.ActivationFunctionType
+ALU = mybir.AluOpType
+
+P = 128
+PACK = 4
+PASSES = 2
+BANK = 512
+CHUNKS = S // BANK
+RUN = 8
+HALF = PAIRS // 2
+TAIL = (256, 128, 128)
+
+
+def tile_list_contradiction_finder_scores_kernel(
+    tc, tab_words, tab_scales, offs, pos1, pos2, pos3, pos4, wp, wt_words, wt_scales, gain, wo, out
+):
+    nc = tc.nc
+    with ExitStack() as ctx:
+        keep = ctx.enter_context(tc.tile_pool(name="keep", bufs=1))
+        ring = ctx.enter_context(tc.tile_pool(name="ring", bufs=2))
+        psum = ctx.enter_context(tc.psum_pool(name="psum", bufs=1))
+        banks = [psum.tile([P, BANK], F32, name=f"bank{i}") for i in range(8)]
+
+        def load_list(name, src):
+            held = keep.tile(list(src.shape), U16, name=name)
+            nc.sync.dma_start(held[:], src)
+            return held
+
+        offs_t = load_list("offs_t", offs)
+        scale_win = keep.tile([P, T], U8, name="scale_win", align_bytes=64)
+        for q in range(4):
+            nc.sync.dma_start(
+                out=scale_win[32 * q + 24 : 32 * q + 32, :].bitcast(I32),
+                in_=tab_scales[:, 4 * q : 4 * q + 4, :].bitcast(I32),
+            )
+        for q in range(4):
+            nc.vector.memset(scale_win[32 * q : 32 * q + 24, :].bitcast(I32), 0)
+
+        word_win = [keep.tile([P, T], U32, name=f"word_win{a}", align_bytes=64) for a in range(PASSES)]
+
+        def load_words(a):
+            nc.sync.dma_start(
+                out=word_win[a][:].bitcast(I32),
+                in_=tab_words[a].rearrange("p t i -> p (t i)").bitcast(I32),
+            )
+
+        wt_raw = keep.tile([P, PASSES, 2 * H // 4], U32, name="wt_raw", align_bytes=64)
+        nc.sync.dma_start(out=wt_raw[:].bitcast(I32), in_=wt_words.rearrange("a p c -> p a c").bitcast(I32))
+        load_words(0)
+        pos2_t = load_list("pos2_t", pos2)
+        pos4_t = load_list("pos4_t", pos4)
+        pos1_t = load_list("pos1_t", pos1)
+        pos3_t = load_list("pos3_t", pos3)
+        load_words(1)
+
+        w_raw = []
+        for a in range(PASSES):
+            raw = ring.tile([P, PACK, H], F32, name="w_raw")
+            nc.sync.dma_start(out=raw[:], in_=wp[512 * a : 512 * (a + 1), :].rearrange("(p j) r -> p j r", j=PACK))
+            w_raw.append(raw)
+
+        wts_raw = keep.tile([P, PASSES, H // 4], U32, name="wts_raw", align_bytes=64)
+        nc.gpsimd.memset(wts_raw[:], 0)
+        for q in range(4):
+            nc.gpsimd.dma_start(
+                out=wts_raw[32 * q : 32 * q + 4, :, :].bitcast(I32),
+                in_=wt_scales[:, 4 * q : 4 * q + 4, :].rearrange("a r c -> r a c").bitcast(I32),
+            )
+        gains = [keep.tile([P, 1], F32, name=f"gain{t}") for t in range(PACK)]
+        with nc.allow_non_contiguous_dma(reason="one gain to a partition"):
+            for t in range(PACK):
+                nc.gpsimd.dma_start(out=gains[t][:], in_=gain.rearrange("(b t q) -> t b q", t=PACK, q=RUN)[t])
+
+        planes = keep.tile([P, PASSES, S], U8, name="planes", align_bytes=64)
+        for a in range(PASSES):
+            nc.vector.memset(planes[96:128, a, :].bitcast(I32), 0)
+        picked_scales = keep.tile([P, S], U8, name="picked_scales", align_bytes=64)
+        nc.vector.tensor_copy(picked_scales[:], scale_win[:].indirect(offs_t[:]))
+        for a in range(PASSES):
+            shift = 24 + 4 * a
+            nc.scalar.dma_start(
+                out=planes[0:100, a, :].bitcast(I32), in_=picked_scales[shift : shift + 100, :].bitcast(I32)
+            )
+        picked = [keep.tile([P, S], U32, name=f"picked{a}", align_bytes=64) for a in range(PASSES)]
+        nc.vector.tensor_copy(picked[0][:], word_win[0][:].indirect(offs_t[:]))
+        for c in range(CHUNKS):
+            nc.vector.tensor_copy(
+                picked[1][:, BANK * c : BANK * (c + 1)],
+                word_win[1][:].indirect(offs_t[:, 32 * c : 32 * (c + 1)]),
+            )
+
+        wt_codes = keep.tile([P, PASSES, 2 * H], U8, name="wt_codes", align_bytes=64)
+        wt_planes = keep.tile([P, PASSES, H], U8, name="wt_planes", align_bytes=64)
+        for a in range(PASSES):
+            nc.scalar.copy(
+                out=wt_codes[:, a, :].bitcast(U32).rearrange("p (t b w) -> p t b w", t=PACK, w=4),
+                in_=wt_raw[:, a, :].rearrange("p (b t w) -> p t b w", t=PACK, w=4),
+            )
+            nc.scalar.copy(
+                out=wt_planes[:, a, :].bitcast(U32).rearrange("p (t b w) -> p t b w", t=PACK, w=2),
+                in_=wts_raw[:, a, :].rearrange("p (b t w) -> p t b w", t=PACK, w=2),
+            )
+
+        wp_bf = [keep.tile([P, PASSES, P * PACK], BF16, name=f"wp_bf{t}", align_bytes=64) for t in range(PACK)]
+        wp_codes = [keep.tile([P, PASSES, P], U32, name=f"wp_codes{t}", align_bytes=64) for t in range(PACK)]
+        wp_planes = [keep.tile([P, PASSES, P], U8, name=f"wp_planes{t}", align_bytes=64) for t in range(PACK)]
+
+        def quantise_wp(t, copy):
+            for a in range(PASSES):
+                copy(
+                    out=wp_bf[t][:, a, :].rearrange("p (b q j) -> p b q j", q=RUN, j=PACK),
+                    in_=w_raw[a][:].rearrange("p j (b t q) -> p t b q j", t=PACK, q=RUN)[:, t],
+                )
+            nc.vector.quantize_mx(
+                out=wp_codes[t][:].rearrange("p a m -> p (a m)").bitcast(FP8X4),
+                scales=wp_planes[t][:].rearrange("p a m -> p (a m)"),
+                in_=wp_bf[t][:].rearrange("p a m -> p (a m)"),
+            )
+
+        h = [keep.tile([P, S], F32, name=f"h{t}") for t in range(PACK)]
+        bent = [keep.tile([P, S], F32, name=f"bent{t}") for t in range(PACK)]
+
+        def product(bank, c, codes, plane):
+            cols = slice(BANK * c, BANK * (c + 1))
+            for a in range(PASSES):
+                nc.tensor.matmul_mx(
+                    out=bank[:],
+                    lhsT=codes(a),
+                    lhsT_scale=plane(a),
+                    rhs=picked[a][:, cols].bitcast(FP8X4),
+                    rhs_scale=planes[:, a, cols],
+                    start=(a == 0),
+                    stop=(a == PASSES - 1),
+                )
+
+        def tanh_branch(t, c, bank):
+            product(
+                bank,
+                c,
+                lambda a: wt_codes[:, a, 2 * P * t : 2 * P * (t + 1)].bitcast(FP4X4),
+                lambda a: wt_planes[:, a, P * t : P * (t + 1)],
+            )
+            nc.scalar.activation(out=bent[t][:, BANK * c : BANK * (c + 1)], in_=bank[:], func=ACT.Tanh)
+
+        def linear_branch(t, c, bank):
+            product(bank, c, lambda a: wp_codes[t][:, a, :].bitcast(FP8X4), lambda a: wp_planes[t][:, a, :])
+            cols = slice(BANK * c, BANK * (c + 1))
+            nc.vector.tensor_tensor(out=h[t][:, cols], in0=bank[:], in1=bent[t][:, cols], op=ALU.add)
+
+        a2_bf = keep.tile([P, KEPT, PACK], BF16, name="a2_bf", align_bytes=64)
+        a1 = {}
+        exhibit = {}
+
+        def pairs(t):
+            second = ring.tile([P, PAIRS], F32, name="second")
+            factor = ring.tile([P, PAIRS], F32, name="factor")
+            a1[t] = ring.tile([P, PAIRS], F32, name="a1")
+            exhibit[t] = ring.tile([P, KEPT], F32, name="exhibit")
+            for u in range(2):
+                cols = slice(HALF * u, HALF * (u + 1))
+                nc.vector.tensor_copy(second[:, cols], h[t][:].indirect(pos2_t[:, 32 * u : 32 * (u + 1)]))
+                nc.scalar.activation(out=second[:, cols], in_=second[:, cols], func=ACT.Tanh)
+                nc.scalar.activation(out=factor[:, cols], in_=second[:, cols], func=ACT.Identity, bias=1.0)
+            nc.vector.tensor_copy(exhibit[t][:], h[t][:].indirect(pos4_t[:]))
+            for u in range(2):
+                cols = slice(HALF * u, HALF * (u + 1))
+                nc.vector.tensor_tensor(
+                    out=a1[t][:, cols],
+                    in0=h[t][:].indirect(pos1_t[:, 32 * u : 32 * (u + 1)]),
+                    in1=factor[:, cols],
+                    op=ALU.mult,
+                )
+
+        def compare(t, j0, width):
+            cols = slice(j0, j0 + width)
+            kept = ring.tile([P, KEPT], F32, name="kept")
+            larger = ring.tile([P, KEPT], F32, name="larger")
+            nc.vector.tensor_copy(kept[:, :width], a1[t][:].indirect(pos3_t[:, j0 // 16 : (j0 + width) // 16]))
+            nc.vector.tensor_tensor(out=larger[:, :width], in0=kept[:, :width], in1=exhibit[t][:, cols], op=ALU.max)
+            nc.scalar.activation(
+                out=a2_bf[:, cols, t], in_=larger[:, :width], func=ACT.Copy, scale=gains[t][:]
+            )
+
+        wo_bf = keep.tile([P, N, PACK], BF16, name="wo_bf", align_bytes=64)
+        wo_codes = keep.tile([P, N], U32, name="wo_codes", align_bytes=64)
+        wo_plane = keep.tile([P, N], U8, name="wo_plane", align_bytes=64)
+
+        def quantise_wo():
+            raw = ring.tile([P, PACK, N], F32, name="w_raw")
+            rows = wo.rearrange("(b t q) n -> t b q n", t=PACK, q=RUN)
+            for t in range(PACK):
+                nc.sync.dma_start(out=raw[:, t, :], in_=rows[t])
+            nc.scalar.copy(out=wo_bf[:], in_=raw[:].rearrange("p t n -> p n t"))
+            nc.vector.quantize_mx(
+                out=wo_codes[:].bitcast(FP8X4), scales=wo_plane[:], in_=wo_bf[:].rearrange("p n t -> p (n t)")
+            )
+
+        a2_codes = keep.tile([P, KEPT], U32, name="a2_codes", align_bytes=64)
+        a2_plane = keep.tile([P, KEPT], U8, name="a2_plane", align_bytes=64)
+        out_rows = out.rearrange("(g p) j -> p g j", p=P)
+
+        def scores(j0, width, pair):
+            cols = slice(j0, j0 + width)
+            nc.vector.quantize_mx(
+                out=a2_codes[:, cols].bitcast(FP8X4),
+                scales=a2_plane[:, cols],
+                in_=a2_bf[:, cols, :].rearrange("p j t -> p (j t)"),
+            )
+            result = keep.tile([P, 4, width], F32, name=f"result{j0}")
+            for half, copy in enumerate((nc.scalar.copy, nc.vector.tensor_copy)):
+                for i in range(2):
+                    g = 2 * half + i
+                    nc.tensor.matmul_mx(
+                        out=pair[half][:, width * i : width * (i + 1)],
+                        lhsT=wo_codes[:, P * g : P * (g + 1)].bitcast(FP8X4),
+                        lhsT_scale=wo_plane[:, P * g : P * (g + 1)],
+                        rhs=a2_codes[:, cols].bitcast(FP8X4),
+                        rhs_scale=a2_plane[:, cols],
+                        start=True,
+                        stop=True,
+                    )
+                copy(
+                    out=result[:, 2 * half : 2 * half + 2, :].rearrange("p g j -> p (g j)"),
+                    in_=pair[half][:, : 2 * width],
+                )
+            nc.sync.dma_start(out=out_rows[:, :, cols], in_=result[:])
+
+        low, high = banks[:4], banks[4:]
+        quantise_wp(0, nc.vector.tensor_copy)
+        for c in range(CHUNKS):
+            tanh_branch(0, c, low[(2 * c) % 4])
+            tanh_branch(1, c, low[(2 * c + 1) % 4])
+        for c in range(CHUNKS):
+            linear_branch(0, c, high[c])
+        quantise_wp(1, nc.scalar.copy)
+        pairs(0)
+        for c in range(CHUNKS):
+            linear_branch(1, c, low[c])
+        quantise_wp(2, nc.scalar.copy)
+        quantise_wp(3, nc.scalar.copy)
+        for c in range(CHUNKS):
+            tanh_branch(2, c, high[c])
+        compare(0, 0, KEPT)
+        pairs(1)
+        for c in range(CHUNKS):
+            tanh_branch(3, c, high[c])
+        for c in range(CHUNKS):
+            linear_branch(2, c, low[c])
+        quantise_wo()
+        compare(1, 0, KEPT)
+        pairs(2)
+        for c in range(CHUNKS):
+            linear_branch(3, c, high[c])
+        compare(2, 0, KEPT)
+        pairs(3)
+        j0 = 0
+        for i, width in enumerate(TAIL):
+            compare(3, j0, width)
+            scores(j0, width, banks[2 * i : 2 * i + 2])
+            j0 = j0 + width

@@ -1,6 +1,7 @@
 from contextlib import ExitStack
 
 import concourse.mybir as mybir
+from concourse.masks import make_identity
 
 K, H, N, T, S, PAIRS, KEPT = 1024, 512, 512, 4096, 2048, 1024, 512
 FLOPS = 2 * 2 * K * H * S + 2 * H * N * KEPT
@@ -33,6 +34,7 @@ def tile_list_contradiction_finder_scores_kernel(
     with ExitStack() as ctx:
         keep = ctx.enter_context(tc.tile_pool(name="keep", bufs=1))
         ring = ctx.enter_context(tc.tile_pool(name="ring", bufs=2))
+        four = ctx.enter_context(tc.tile_pool(name="four", bufs=4))
         psum = ctx.enter_context(tc.psum_pool(name="psum", bufs=1))
         banks = [psum.tile([P, BANK], F32, name=f"bank{i}") for i in range(8)]
 
@@ -43,13 +45,10 @@ def tile_list_contradiction_finder_scores_kernel(
 
         offs_t = load_list("offs_t", offs)
         scale_win = keep.tile([P, T], U8, name="scale_win", align_bytes=64)
-        for q in range(4):
-            nc.sync.dma_start(
-                out=scale_win[32 * q + 24 : 32 * q + 32, :].bitcast(I32),
-                in_=tab_scales[:, 4 * q : 4 * q + 4, :].bitcast(I32),
-            )
-        for q in range(4):
-            nc.vector.memset(scale_win[32 * q : 32 * q + 24, :].bitcast(I32), 0)
+        nc.sync.dma_start(
+            out=scale_win[96:128, :].bitcast(I32), in_=tab_scales.rearrange("a q t -> (a q) t").bitcast(I32)
+        )
+        nc.vector.memset(scale_win[0:96, :].bitcast(I32), 0)
 
         word_win = [keep.tile([P, T], U32, name=f"word_win{a}", align_bytes=64) for a in range(PASSES)]
 
@@ -62,42 +61,43 @@ def tile_list_contradiction_finder_scores_kernel(
         wt_raw = keep.tile([P, PASSES, 2 * H // 4], U32, name="wt_raw", align_bytes=64)
         nc.sync.dma_start(out=wt_raw[:].bitcast(I32), in_=wt_words.rearrange("a p c -> p a c").bitcast(I32))
         load_words(0)
+        load_words(1)
+        wp_raw = keep.tile([P, PASSES, PACK, H], F32, name="wp_raw", tag="raw", align_bytes=64)
+        nc.sync.dma_start(out=wp_raw[:], in_=wp.rearrange("(a p j) r -> p a j r", a=PASSES, j=PACK))
         pos2_t = load_list("pos2_t", pos2)
         pos4_t = load_list("pos4_t", pos4)
         pos1_t = load_list("pos1_t", pos1)
         pos3_t = load_list("pos3_t", pos3)
-        load_words(1)
 
-        w_raw = []
-        for a in range(PASSES):
-            raw = ring.tile([P, PACK, H], F32, name="w_raw")
-            nc.sync.dma_start(out=raw[:], in_=wp[512 * a : 512 * (a + 1), :].rearrange("(p j) r -> p j r", j=PACK))
-            w_raw.append(raw)
 
-        wts_raw = keep.tile([P, PASSES, H // 4], U32, name="wts_raw", align_bytes=64)
+        wts_raw = keep.tile([P, PASSES, H // 4], U32, name="wts_raw")
         nc.gpsimd.memset(wts_raw[:], 0)
         for q in range(4):
             nc.gpsimd.dma_start(
                 out=wts_raw[32 * q : 32 * q + 4, :, :].bitcast(I32),
                 in_=wt_scales[:, 4 * q : 4 * q + 4, :].rearrange("a r c -> r a c").bitcast(I32),
             )
-        gains = [keep.tile([P, 1], F32, name=f"gain{t}") for t in range(PACK)]
-        with nc.allow_non_contiguous_dma(reason="one gain to a partition"):
-            for t in range(PACK):
-                nc.gpsimd.dma_start(out=gains[t][:], in_=gain.rearrange("(b t q) -> t b q", t=PACK, q=RUN)[t])
+        ident = keep.tile([P, P], F32, name="ident")
+        make_identity(nc, ident[:])
 
         planes = keep.tile([P, PASSES, S], U8, name="planes", align_bytes=64)
-        for a in range(PASSES):
-            nc.vector.memset(planes[96:128, a, :].bitcast(I32), 0)
+        nc.vector.memset(planes[:].rearrange("p a s -> p (a s)").bitcast(I32), 0)
         picked_scales = keep.tile([P, S], U8, name="picked_scales", align_bytes=64)
         nc.vector.tensor_copy(picked_scales[:], scale_win[:].indirect(offs_t[:]))
         for a in range(PASSES):
-            shift = 24 + 4 * a
-            nc.scalar.dma_start(
-                out=planes[0:100, a, :].bitcast(I32), in_=picked_scales[shift : shift + 100, :].bitcast(I32)
-            )
+            for q in range(4):
+                row = 96 + 16 * a + 4 * q
+                queue = nc.gpsimd if q == 3 else nc.scalar
+                queue.dma_start(
+                    out=planes[32 * q : 32 * q + 4, a, :].bitcast(I32),
+                    in_=picked_scales[row : row + 4, :].bitcast(I32),
+                )
         picked = [keep.tile([P, S], U32, name=f"picked{a}", align_bytes=64) for a in range(PASSES)]
-        nc.vector.tensor_copy(picked[0][:], word_win[0][:].indirect(offs_t[:]))
+        for u in range(2):
+            nc.vector.tensor_copy(
+                picked[0][:, S // 2 * u : S // 2 * (u + 1)],
+                word_win[0][:].indirect(offs_t[:, 64 * u : 64 * (u + 1)]),
+            )
         for c in range(CHUNKS):
             nc.vector.tensor_copy(
                 picked[1][:, BANK * c : BANK * (c + 1)],
@@ -116,24 +116,34 @@ def tile_list_contradiction_finder_scores_kernel(
                 in_=wts_raw[:, a, :].rearrange("p (b t w) -> p t b w", t=PACK, w=2),
             )
 
-        wp_bf = [keep.tile([P, PASSES, P * PACK], BF16, name=f"wp_bf{t}", align_bytes=64) for t in range(PACK)]
-        wp_codes = [keep.tile([P, PASSES, P], U32, name=f"wp_codes{t}", align_bytes=64) for t in range(PACK)]
-        wp_planes = [keep.tile([P, PASSES, P], U8, name=f"wp_planes{t}", align_bytes=64) for t in range(PACK)]
 
-        def quantise_wp(t, copy):
+        wp_codes = {}
+        wp_planes = {}
+
+        def quantise_wp(t0, count, copy):
+            rounded = keep.tile([P, PASSES, count, P * PACK], BF16, name=f"wp_bf{t0}", tag=f"rounded{t0}", align_bytes=64)
+            wp_codes[t0] = keep.tile([P, PASSES, count * P], U32, name=f"wp_codes{t0}", align_bytes=64)
+            wp_planes[t0] = keep.tile([P, PASSES, count * P], U8, name=f"wp_planes{t0}", align_bytes=64)
             for a in range(PASSES):
-                copy(
-                    out=wp_bf[t][:, a, :].rearrange("p (b q j) -> p b q j", q=RUN, j=PACK),
-                    in_=w_raw[a][:].rearrange("p j (b t q) -> p t b q j", t=PACK, q=RUN)[:, t],
-                )
+                for i in range(count):
+                    copy(
+                        out=rounded[:, a, i, :].rearrange("p (b q j) -> p b q j", q=RUN, j=PACK),
+                        in_=wp_raw[:, a, :, :].rearrange("p j (b t q) -> p t b q j", t=PACK, q=RUN)[:, t0 + i],
+                    )
             nc.vector.quantize_mx(
-                out=wp_codes[t][:].rearrange("p a m -> p (a m)").bitcast(FP8X4),
-                scales=wp_planes[t][:].rearrange("p a m -> p (a m)"),
-                in_=wp_bf[t][:].rearrange("p a m -> p (a m)"),
+                out=wp_codes[t0][:].rearrange("p a m -> p (a m)").bitcast(FP8X4),
+                scales=wp_planes[t0][:].rearrange("p a m -> p (a m)"),
+                in_=rounded[:].rearrange("p a i m -> p (a i m)"),
             )
 
         h = [keep.tile([P, S], F32, name=f"h{t}") for t in range(PACK)]
-        bent = [keep.tile([P, S], F32, name=f"bent{t}") for t in range(PACK)]
+        first = keep.tile([P, 2 * BANK], F32, name="bent_first", tag="rounded2", align_bytes=64)
+        third = keep.tile([P, BANK], F32, name="bent_third", tag="rounded1", align_bytes=64)
+        others = keep.tile([P, 5, BANK], F32, name="bent_others")
+        bent = [
+            [third[:], first[:, :BANK], first[:, BANK:], others[:, 4, :]],
+            [others[:, c, :] for c in range(CHUNKS)],
+        ]
 
         def product(bank, c, codes, plane):
             cols = slice(BANK * c, BANK * (c + 1))
@@ -155,14 +165,63 @@ def tile_list_contradiction_finder_scores_kernel(
                 lambda a: wt_codes[:, a, 2 * P * t : 2 * P * (t + 1)].bitcast(FP4X4),
                 lambda a: wt_planes[:, a, P * t : P * (t + 1)],
             )
-            nc.scalar.activation(out=bent[t][:, BANK * c : BANK * (c + 1)], in_=bank[:], func=ACT.Tanh)
+            nc.scalar.activation(out=bent[t][c], in_=bank[:], func=ACT.Tanh)
 
         def linear_branch(t, c, bank):
             product(bank, c, lambda a: wp_codes[t][:, a, :].bitcast(FP8X4), lambda a: wp_planes[t][:, a, :])
             cols = slice(BANK * c, BANK * (c + 1))
-            nc.vector.tensor_tensor(out=h[t][:, cols], in0=bank[:], in1=bent[t][:, cols], op=ALU.add)
+            nc.vector.tensor_tensor(out=h[t][:, cols], in0=bank[:], in1=bent[t][c], op=ALU.add)
 
-        a2_bf = keep.tile([P, KEPT, PACK], BF16, name="a2_bf", align_bytes=64)
+        WIDE = 2 * P
+        turned_tanh = {}
+        turned_linear = {}
+
+        def turned_product(i, bank, codes, plane):
+            for u in range(2):
+                cols = slice(P * (2 * i + u), P * (2 * i + u + 1))
+                for a in range(PASSES):
+                    nc.tensor.matmul_mx(
+                        out=bank[:, WIDE * u : WIDE * (u + 1)],
+                        lhsT=picked[a][:, cols].bitcast(FP8X4),
+                        lhsT_scale=planes[:, a, cols],
+                        rhs=codes(a),
+                        rhs_scale=plane(a),
+                        start=(a == 0),
+                        stop=(a == PASSES - 1),
+                    )
+
+        def turned_tanh_branch(i, bank):
+            turned_product(
+                i, bank, lambda a: wt_codes[:, a, 2 * WIDE :].bitcast(FP4X4), lambda a: wt_planes[:, a, WIDE:]
+            )
+            turned_tanh[i] = keep.tile([P, BANK], F32, name=f"turned_tanh{i}")
+            nc.scalar.activation(out=turned_tanh[i][:], in_=bank[:], func=ACT.Tanh)
+
+        def turned_linear_branch(i, bank):
+            turned_product(i, bank, lambda a: wp_codes[2][:, a, :].bitcast(FP8X4), lambda a: wp_planes[2][:, a, :])
+            if i % 2 == 0:
+                turned_linear[i // 2] = keep.tile(
+                    [P, 2, BANK], F32, name="turned_linear", tag=f"late{i // 2}", align_bytes=64
+                )
+            nc.scalar.copy(out=turned_linear[i // 2][:, i % 2, :], in_=bank[:])
+
+        def turn_back(t, c, bank):
+            for k in range(4):
+                cols = slice(WIDE * (k % 2) + P * (t - 2), WIDE * (k % 2) + P * (t - 1))
+                parts = (turned_linear[c][:, k // 2, cols], turned_tanh[2 * c + k // 2][:, cols])
+                for e, part in enumerate(parts):
+                    nc.tensor.matmul(
+                        out=bank[:, P * k : P * (k + 1)],
+                        lhsT=part,
+                        rhs=ident[:],
+                        is_transpose=True,
+                        start=(e == 0),
+                        stop=(e == 1),
+                    )
+            nc.scalar.copy(out=h[t][:, BANK * c : BANK * (c + 1)], in_=bank[:])
+
+        late = {}
+        larger = {}
         a1 = {}
         exhibit = {}
 
@@ -189,19 +248,25 @@ def tile_list_contradiction_finder_scores_kernel(
         def compare(t, j0, width):
             cols = slice(j0, j0 + width)
             kept = ring.tile([P, KEPT], F32, name="kept")
-            larger = ring.tile([P, KEPT], F32, name="larger")
+            if j0 == 0:
+                larger[t] = four.tile([P, KEPT], F32, name="larger")
             nc.vector.tensor_copy(kept[:, :width], a1[t][:].indirect(pos3_t[:, j0 // 16 : (j0 + width) // 16]))
-            nc.vector.tensor_tensor(out=larger[:, :width], in0=kept[:, :width], in1=exhibit[t][:, cols], op=ALU.max)
+            nc.vector.tensor_tensor(out=larger[t][:, cols], in0=kept[:, :width], in1=exhibit[t][:, cols], op=ALU.max)
+
+        def apply_gain(t, j0, width):
+            cols = slice(j0, j0 + width)
+            if "a2" not in late:
+                late["a2"] = keep.tile([P, KEPT, PACK], BF16, name="a2_bf", tag="late0", align_bytes=64)
             nc.scalar.activation(
-                out=a2_bf[:, cols, t], in_=larger[:, :width], func=ACT.Copy, scale=gains[t][:]
+                out=late["a2"][:, cols, t], in_=larger[t][:, cols], func=ACT.Copy, scale=gains[:, t, 0:1]
             )
 
-        wo_bf = keep.tile([P, N, PACK], BF16, name="wo_bf", align_bytes=64)
         wo_codes = keep.tile([P, N], U32, name="wo_codes", align_bytes=64)
         wo_plane = keep.tile([P, N], U8, name="wo_plane", align_bytes=64)
 
         def quantise_wo():
-            raw = ring.tile([P, PACK, N], F32, name="w_raw")
+            raw = keep.tile([P, PACK, N], F32, name="wo_raw", tag="raw", align_bytes=64)
+            wo_bf = keep.tile([P, N, PACK], BF16, name="wo_bf", tag="late1", align_bytes=64)
             rows = wo.rearrange("(b t q) n -> t b q n", t=PACK, q=RUN)
             for t in range(PACK):
                 nc.sync.dma_start(out=raw[:, t, :], in_=rows[t])
@@ -219,7 +284,7 @@ def tile_list_contradiction_finder_scores_kernel(
             nc.vector.quantize_mx(
                 out=a2_codes[:, cols].bitcast(FP8X4),
                 scales=a2_plane[:, cols],
-                in_=a2_bf[:, cols, :].rearrange("p j t -> p (j t)"),
+                in_=late["a2"][:, cols, :].rearrange("p j t -> p (j t)"),
             )
             result = keep.tile([P, 4, width], F32, name=f"result{j0}")
             for half, copy in enumerate((nc.scalar.copy, nc.vector.tensor_copy)):
@@ -241,35 +306,45 @@ def tile_list_contradiction_finder_scores_kernel(
             nc.sync.dma_start(out=out_rows[:, :, cols], in_=result[:])
 
         low, high = banks[:4], banks[4:]
-        quantise_wp(0, nc.vector.tensor_copy)
+        quantise_wp(0, 1, nc.vector.tensor_copy)
+        gains = keep.tile([P, PACK, 8], F32, name="gains", tag="rounded0", align_bytes=64)
+        with nc.allow_non_contiguous_dma(reason="one gain to a partition"):
+            for t in range(PACK):
+                nc.sync.dma_start(out=gains[:, t, 0:1], in_=gain.rearrange("(b t q) -> t b q", t=PACK, q=RUN)[t])
         for c in range(CHUNKS):
-            tanh_branch(0, c, low[(2 * c) % 4])
-            tanh_branch(1, c, low[(2 * c + 1) % 4])
+            tanh_branch(0, c, banks[2 * c])
+            tanh_branch(1, c, banks[2 * c + 1])
         for c in range(CHUNKS):
-            linear_branch(0, c, high[c])
-        quantise_wp(1, nc.scalar.copy)
+            linear_branch(0, c, low[c])
+        quantise_wp(1, 1, nc.scalar.copy)
+        quantise_wp(2, 2, nc.scalar.copy)
         pairs(0)
-        for c in range(CHUNKS):
-            linear_branch(1, c, low[c])
-        quantise_wp(2, nc.scalar.copy)
-        quantise_wp(3, nc.scalar.copy)
-        for c in range(CHUNKS):
-            tanh_branch(2, c, high[c])
+        for c in range(CHUNKS - 1):
+            linear_branch(1, c, high[c])
         compare(0, 0, KEPT)
+        free = low + [high[3]]
+        for i in range(8):
+            turned_tanh_branch(i, free[i % 5])
+        linear_branch(1, CHUNKS - 1, free[7 % 5])
         pairs(1)
+        rest = [free[(8 + i) % 5] for i in range(4)]
+        for i in range(8):
+            turned_linear_branch(i, rest[i % 4])
         for c in range(CHUNKS):
-            tanh_branch(3, c, high[c])
-        for c in range(CHUNKS):
-            linear_branch(2, c, low[c])
-        quantise_wo()
+            turn_back(2, c, high[c % 3])
         compare(1, 0, KEPT)
         pairs(2)
         for c in range(CHUNKS):
-            linear_branch(3, c, high[c])
+            turn_back(3, c, high[(c + 1) % 3])
+        apply_gain(0, 0, KEPT)
+        apply_gain(1, 0, KEPT)
+        quantise_wo()
         compare(2, 0, KEPT)
         pairs(3)
+        apply_gain(2, 0, KEPT)
         j0 = 0
         for i, width in enumerate(TAIL):
             compare(3, j0, width)
+            apply_gain(3, j0, width)
             scores(j0, width, banks[2 * i : 2 * i + 2])
             j0 = j0 + width

from contextlib import ExitStack

import concourse.mybir as mybir
from concourse.masks import make_identity

K, H, N, T, S, PAIRS, KEPT = 1024, 512, 512, 4096, 2048, 1024, 512
FLOPS = 2 * 2 * K * H * S + 2 * H * N * KEPT

F32 = mybir.dt.float32
BF16 = mybir.dt.bfloat16
I32 = mybir.dt.int32
U32 = mybir.dt.uint32
U16 = mybir.dt.uint16
U8 = mybir.dt.uint8
FP8X4 = mybir.dt.float8_e4m3fn_x4
FP4X4 = mybir.dt.float4_e2m1fn_x4
ACT = mybir.ActivationFunctionType
ALU = mybir.AluOpType

P = 128
PACK = 4
PASSES = 2
BANK = 512
CHUNKS = S // BANK
RUN = 8
HALF = PAIRS // 2
TAIL = (256, 128, 128)


def tile_list_contradiction_finder_scores_kernel(
    tc, tab_words, tab_scales, offs, pos1, pos2, pos3, pos4, wp, wt_words, wt_scales, gain, wo, out
):
    nc = tc.nc
    with ExitStack() as ctx:
        keep = ctx.enter_context(tc.tile_pool(name="keep", bufs=1))
        ring = ctx.enter_context(tc.tile_pool(name="ring", bufs=2))
        four = ctx.enter_context(tc.tile_pool(name="four", bufs=4))
        psum = ctx.enter_context(tc.psum_pool(name="psum", bufs=1))
        banks = [psum.tile([P, BANK], F32, name=f"bank{i}") for i in range(8)]

        def load_list(name, src):
            held = keep.tile(list(src.shape), U16, name=name)
            nc.sync.dma_start(held[:], src)
            return held

        offs_t = load_list("offs_t", offs)
        scale_win = keep.tile([P, T], U8, name="scale_win", align_bytes=64)
        nc.sync.dma_start(
            out=scale_win[96:128, :].bitcast(I32), in_=tab_scales.rearrange("a q t -> (a q) t").bitcast(I32)
        )
        nc.vector.memset(scale_win[0:96, :].bitcast(I32), 0)

        word_win = [keep.tile([P, T], U32, name=f"word_win{a}", align_bytes=64) for a in range(PASSES)]

        def load_words(a):
            nc.sync.dma_start(
                out=word_win[a][:].bitcast(I32),
                in_=tab_words[a].rearrange("p t i -> p (t i)").bitcast(I32),
            )

        wt_raw = keep.tile([P, PASSES, 2 * H // 4], U32, name="wt_raw", align_bytes=64)
        nc.sync.dma_start(out=wt_raw[:].bitcast(I32), in_=wt_words.rearrange("a p c -> p a c").bitcast(I32))
        load_words(0)
        load_words(1)
        wp_raw = keep.tile([P, PASSES, PACK, H], F32, name="wp_raw", tag="raw", align_bytes=64)
        nc.sync.dma_start(out=wp_raw[:], in_=wp.rearrange("(a p j) r -> p a j r", a=PASSES, j=PACK))
        pos2_t = load_list("pos2_t", pos2)
        pos4_t = load_list("pos4_t", pos4)
        pos1_t = load_list("pos1_t", pos1)
        pos3_t = load_list("pos3_t", pos3)


        wts_raw = keep.tile([P, PASSES, H // 4], U32, name="wts_raw")
        nc.gpsimd.memset(wts_raw[:], 0)
        for q in range(4):
            nc.gpsimd.dma_start(
                out=wts_raw[32 * q : 32 * q + 4, :, :].bitcast(I32),
                in_=wt_scales[:, 4 * q : 4 * q + 4, :].rearrange("a r c -> r a c").bitcast(I32),
            )
        ident = keep.tile([P, P], F32, name="ident")
        make_identity(nc, ident[:])

        planes = keep.tile([P, PASSES, S], U8, name="planes", align_bytes=64)
        nc.vector.memset(planes[:].rearrange("p a s -> p (a s)").bitcast(I32), 0)
        picked_scales = keep.tile([P, S], U8, name="picked_scales", align_bytes=64)
        nc.vector.tensor_copy(picked_scales[:], scale_win[:].indirect(offs_t[:]))
        for a in range(PASSES):
            for q in range(4):
                row = 96 + 16 * a + 4 * q
                queue = nc.gpsimd if q == 3 else nc.scalar
                queue.dma_start(
                    out=planes[32 * q : 32 * q + 4, a, :].bitcast(I32),
                    in_=picked_scales[row : row + 4, :].bitcast(I32),
                )
        picked = [keep.tile([P, S], U32, name=f"picked{a}", align_bytes=64) for a in range(PASSES)]
        for u in range(2):
            nc.vector.tensor_copy(
                picked[0][:, S // 2 * u : S // 2 * (u + 1)],
                word_win[0][:].indirect(offs_t[:, 64 * u : 64 * (u + 1)]),
            )
        for c in range(CHUNKS):
            nc.vector.tensor_copy(
                picked[1][:, BANK * c : BANK * (c + 1)],
                word_win[1][:].indirect(offs_t[:, 32 * c : 32 * (c + 1)]),
            )

        wt_codes = keep.tile([P, PASSES, 2 * H], U8, name="wt_codes", align_bytes=64)
        wt_planes = keep.tile([P, PASSES, H], U8, name="wt_planes", align_bytes=64)
        for a in range(PASSES):
            nc.scalar.copy(
                out=wt_codes[:, a, :].bitcast(U32).rearrange("p (t b w) -> p t b w", t=PACK, w=4),
                in_=wt_raw[:, a, :].rearrange("p (b t w) -> p t b w", t=PACK, w=4),
            )
            nc.scalar.copy(
                out=wt_planes[:, a, :].bitcast(U32).rearrange("p (t b w) -> p t b w", t=PACK, w=2),
                in_=wts_raw[:, a, :].rearrange("p (b t w) -> p t b w", t=PACK, w=2),
            )


        wp_codes = {}
        wp_planes = {}

        def quantise_wp(t0, count, copy):
            rounded = keep.tile([P, PASSES, count, P * PACK], BF16, name=f"wp_bf{t0}", tag=f"rounded{t0}", align_bytes=64)
            wp_codes[t0] = keep.tile([P, PASSES, count * P], U32, name=f"wp_codes{t0}", align_bytes=64)
            wp_planes[t0] = keep.tile([P, PASSES, count * P], U8, name=f"wp_planes{t0}", align_bytes=64)
            for a in range(PASSES):
                for i in range(count):
                    copy(
                        out=rounded[:, a, i, :].rearrange("p (b q j) -> p b q j", q=RUN, j=PACK),
                        in_=wp_raw[:, a, :, :].rearrange("p j (b t q) -> p t b q j", t=PACK, q=RUN)[:, t0 + i],
                    )
            nc.vector.quantize_mx(
                out=wp_codes[t0][:].rearrange("p a m -> p (a m)").bitcast(FP8X4),
                scales=wp_planes[t0][:].rearrange("p a m -> p (a m)"),
                in_=rounded[:].rearrange("p a i m -> p (a i m)"),
            )

        h = [keep.tile([P, S], F32, name=f"h{t}") for t in range(PACK)]
        first = keep.tile([P, 2 * BANK], F32, name="bent_first", tag="rounded2", align_bytes=64)
        third = keep.tile([P, BANK], F32, name="bent_third", tag="rounded1", align_bytes=64)
        others = keep.tile([P, 5, BANK], F32, name="bent_others")
        bent = [
            [third[:], first[:, :BANK], first[:, BANK:], others[:, 4, :]],
            [others[:, c, :] for c in range(CHUNKS)],
        ]

        def product(bank, c, codes, plane):
            cols = slice(BANK * c, BANK * (c + 1))
            for a in range(PASSES):
                nc.tensor.matmul_mx(
                    out=bank[:],
                    lhsT=codes(a),
                    lhsT_scale=plane(a),
                    rhs=picked[a][:, cols].bitcast(FP8X4),
                    rhs_scale=planes[:, a, cols],
                    start=(a == 0),
                    stop=(a == PASSES - 1),
                )

        def tanh_branch(t, c, bank):
            product(
                bank,
                c,
                lambda a: wt_codes[:, a, 2 * P * t : 2 * P * (t + 1)].bitcast(FP4X4),
                lambda a: wt_planes[:, a, P * t : P * (t + 1)],
            )
            nc.scalar.activation(out=bent[t][c], in_=bank[:], func=ACT.Tanh)

        def linear_branch(t, c, bank):
            product(bank, c, lambda a: wp_codes[t][:, a, :].bitcast(FP8X4), lambda a: wp_planes[t][:, a, :])
            cols = slice(BANK * c, BANK * (c + 1))
            nc.vector.tensor_tensor(out=h[t][:, cols], in0=bank[:], in1=bent[t][c], op=ALU.add)

        WIDE = 2 * P
        turned_tanh = {}
        turned_linear = {}

        def turned_product(i, bank, codes, plane):
            for u in range(2):
                cols = slice(P * (2 * i + u), P * (2 * i + u + 1))
                for a in range(PASSES):
                    nc.tensor.matmul_mx(
                        out=bank[:, WIDE * u : WIDE * (u + 1)],
                        lhsT=picked[a][:, cols].bitcast(FP8X4),
                        lhsT_scale=planes[:, a, cols],
                        rhs=codes(a),
                        rhs_scale=plane(a),
                        start=(a == 0),
                        stop=(a == PASSES - 1),
                    )

        def turned_tanh_branch(i, bank):
            turned_product(
                i, bank, lambda a: wt_codes[:, a, 2 * WIDE :].bitcast(FP4X4), lambda a: wt_planes[:, a, WIDE:]
            )
            turned_tanh[i] = keep.tile([P, BANK], F32, name=f"turned_tanh{i}")
            nc.scalar.activation(out=turned_tanh[i][:], in_=bank[:], func=ACT.Tanh)

        def turned_linear_branch(i, bank):
            turned_product(i, bank, lambda a: wp_codes[2][:, a, :].bitcast(FP8X4), lambda a: wp_planes[2][:, a, :])
            if i % 2 == 0:
                turned_linear[i // 2] = keep.tile(
                    [P, 2, BANK], F32, name="turned_linear", tag=f"late{i // 2}", align_bytes=64
                )
            nc.scalar.copy(out=turned_linear[i // 2][:, i % 2, :], in_=bank[:])

        def turn_back(t, c, bank):
            for k in range(4):
                cols = slice(WIDE * (k % 2) + P * (t - 2), WIDE * (k % 2) + P * (t - 1))
                parts = (turned_linear[c][:, k // 2, cols], turned_tanh[2 * c + k // 2][:, cols])
                for e, part in enumerate(parts):
                    nc.tensor.matmul(
                        out=bank[:, P * k : P * (k + 1)],
                        lhsT=part,
                        rhs=ident[:],
                        is_transpose=True,
                        start=(e == 0),
                        stop=(e == 1),
                    )
            nc.scalar.copy(out=h[t][:, BANK * c : BANK * (c + 1)], in_=bank[:])

        late = {}
        larger = {}
        a1 = {}
        exhibit = {}

        def pairs(t):
            second = ring.tile([P, PAIRS], F32, name="second")
            factor = ring.tile([P, PAIRS], F32, name="factor")
            a1[t] = ring.tile([P, PAIRS], F32, name="a1")
            exhibit[t] = ring.tile([P, KEPT], F32, name="exhibit")
            for u in range(2):
                cols = slice(HALF * u, HALF * (u + 1))
                nc.vector.tensor_copy(second[:, cols], h[t][:].indirect(pos2_t[:, 32 * u : 32 * (u + 1)]))
                nc.scalar.activation(out=second[:, cols], in_=second[:, cols], func=ACT.Tanh)
                nc.scalar.activation(out=factor[:, cols], in_=second[:, cols], func=ACT.Identity, bias=1.0)
            nc.vector.tensor_copy(exhibit[t][:], h[t][:].indirect(pos4_t[:]))
            for u in range(2):
                cols = slice(HALF * u, HALF * (u + 1))
                nc.vector.tensor_tensor(
                    out=a1[t][:, cols],
                    in0=h[t][:].indirect(pos1_t[:, 32 * u : 32 * (u + 1)]),
                    in1=factor[:, cols],
                    op=ALU.mult,
                )

        def compare(t, j0, width):
            cols = slice(j0, j0 + width)
            kept = ring.tile([P, KEPT], F32, name="kept")
            if j0 == 0:
                larger[t] = four.tile([P, KEPT], F32, name="larger")
            nc.vector.tensor_copy(kept[:, :width], a1[t][:].indirect(pos3_t[:, j0 // 16 : (j0 + width) // 16]))
            nc.vector.tensor_tensor(out=larger[t][:, cols], in0=kept[:, :width], in1=exhibit[t][:, cols], op=ALU.max)

        def apply_gain(t, j0, width):
            cols = slice(j0, j0 + width)
            if "a2" not in late:
                late["a2"] = keep.tile([P, KEPT, PACK], BF16, name="a2_bf", tag="late0", align_bytes=64)
            nc.scalar.activation(
                out=late["a2"][:, cols, t], in_=larger[t][:, cols], func=ACT.Copy, scale=gains[:, t, 0:1]
            )

        wo_codes = keep.tile([P, N], U32, name="wo_codes", align_bytes=64)
        wo_plane = keep.tile([P, N], U8, name="wo_plane", align_bytes=64)

        def quantise_wo():
            raw = keep.tile([P, PACK, N], F32, name="wo_raw", tag="raw", align_bytes=64)
            wo_bf = keep.tile([P, N, PACK], BF16, name="wo_bf", tag="late1", align_bytes=64)
            rows = wo.rearrange("(b t q) n -> t b q n", t=PACK, q=RUN)
            for t in range(PACK):
                nc.sync.dma_start(out=raw[:, t, :], in_=rows[t])
            nc.scalar.copy(out=wo_bf[:], in_=raw[:].rearrange("p t n -> p n t"))
            nc.vector.quantize_mx(
                out=wo_codes[:].bitcast(FP8X4), scales=wo_plane[:], in_=wo_bf[:].rearrange("p n t -> p (n t)")
            )

        a2_codes = keep.tile([P, KEPT], U32, name="a2_codes", align_bytes=64)
        a2_plane = keep.tile([P, KEPT], U8, name="a2_plane", align_bytes=64)
        out_rows = out.rearrange("(g p) j -> p g j", p=P)

        def scores(j0, width, pair):
            cols = slice(j0, j0 + width)
            nc.vector.quantize_mx(
                out=a2_codes[:, cols].bitcast(FP8X4),
                scales=a2_plane[:, cols],
                in_=late["a2"][:, cols, :].rearrange("p j t -> p (j t)"),
            )
            result = keep.tile([P, 4, width], F32, name=f"result{j0}")
            for half, copy in enumerate((nc.scalar.copy, nc.vector.tensor_copy)):
                for i in range(2):
                    g = 2 * half + i
                    nc.tensor.matmul_mx(
                        out=pair[half][:, width * i : width * (i + 1)],
                        lhsT=wo_codes[:, P * g : P * (g + 1)].bitcast(FP8X4),
                        lhsT_scale=wo_plane[:, P * g : P * (g + 1)],
                        rhs=a2_codes[:, cols].bitcast(FP8X4),
                        rhs_scale=a2_plane[:, cols],
                        start=True,
                        stop=True,
                    )
                copy(
                    out=result[:, 2 * half : 2 * half + 2, :].rearrange("p g j -> p (g j)"),
                    in_=pair[half][:, : 2 * width],
                )
            nc.sync.dma_start(out=out_rows[:, :, cols], in_=result[:])

        low, high = banks[:4], banks[4:]
        quantise_wp(0, 1, nc.vector.tensor_copy)
        gains = keep.tile([P, PACK, 8], F32, name="gains", tag="rounded0", align_bytes=64)
        with nc.allow_non_contiguous_dma(reason="one gain to a partition"):
            for t in range(PACK):
                nc.sync.dma_start(out=gains[:, t, 0:1], in_=gain.rearrange("(b t q) -> t b q", t=PACK, q=RUN)[t])
        for c in range(CHUNKS):
            tanh_branch(0, c, banks[2 * c])
            tanh_branch(1, c, banks[2 * c + 1])
        for c in range(CHUNKS):
            linear_branch(0, c, low[c])
        quantise_wp(1, 1, nc.scalar.copy)
        quantise_wp(2, 2, nc.scalar.copy)
        pairs(0)
        for c in range(CHUNKS - 1):
            linear_branch(1, c, high[c])
        compare(0, 0, KEPT)
        free = low + [high[3]]
        for i in range(8):
            turned_tanh_branch(i, free[i % 5])
        linear_branch(1, CHUNKS - 1, free[7 % 5])
        pairs(1)
        rest = [free[(8 + i) % 5] for i in range(4)]
        for i in range(8):
            turned_linear_branch(i, rest[i % 4])
        for c in range(CHUNKS):
            turn_back(2, c, high[c % 3])
        compare(1, 0, KEPT)
        pairs(2)
        for c in range(CHUNKS):
            turn_back(3, c, high[(c + 1) % 3])
        apply_gain(0, 0, KEPT)
        apply_gain(1, 0, KEPT)
        quantise_wo()
        compare(2, 0, KEPT)
        pairs(3)
        apply_gain(2, 0, KEPT)
        j0 = 0
        for i, width in enumerate(TAIL):
            compare(3, j0, width)
            apply_gain(3, j0, width)
            scores(j0, width, banks[2 * i : 2 * i + 2])
            j0 = j0 + width
